import numpy as np, ml_dtypes
CORES = [0,1,2,3,4,5,6,7,24,25,26,27,28,29,30,31,40,41,42,43,44,45,46,47]
N = 24
def setup_inputs(rng):
    return {"x": rng.standard_normal((N, 128, 8), dtype=np.float32).astype(ml_dtypes.bfloat16)}
def reference(x):
    g = np.concatenate(list(x), axis=1)
    return {"y": np.broadcast_to(g, (N,) + g.shape)}

@@ -1,0 +1,59 @@
+from concourse.bass import RemoteDMATransfer, DstId
+
+SCRATCH = {
+    "land": ("sbuf", [128, 192], "bfloat16"),
+}
+SEMAPHORES = ["loaded", "near", "far", "sent", "stored"]
+
+CHIPS = (0, 3, 5)
+SERVES = {2: (0, 1), 3: (2, 3), 6: (4, 5), 7: (6, 7)}
+
+
+def far_targets(core, topo):
+    ch, k = topo.chip(core), core % 8
+    out = []
+    for other in CHIPS:
+        if other == ch:
+            continue
+        if topo.same_plane(ch, other):
+            out.append(other * 8 + k)
+        elif k in SERVES:
+            out.extend(other * 8 + d for d in SERVES[k])
+    return out
+
+
+def rank_program(g, core, T, topo):
+    rank = T.rank_of(core)
+    if rank is None:
+        return
+    S = T.sem
+    ch = topo.chip(core)
+    own = T.land[:, 8 * rank:8 * rank + 8]
+    b = rank // 8
+    block = T.land[:, 64 * b:64 * b + 64]
+
+    def ids(cores):
+        return [DstId(rid=topo.addr(c)[0], pnc=topo.addr(c)[1]) for c in cores]
+
+    g.dma_start(own, T.x[:]).then_inc(S.loaded, 16)
+    g.wait_ge(S.loaded, 16)
+    peers = [c for c in range(ch * 8, ch * 8 + 8) if c != core]
+    g.remote_dma_fused(
+        [RemoteDMATransfer(dst_ids=ids(peers), dma_engine_mask=0xFFFF, remote_sem=S.near,
+                           srcs=[own], dsts=[own] * len(peers), alu_op=0)],
+        local_sem=S.sent)
+    sent = 16
+    g.wait_ge(S.near, 7 * 16)
+
+    tg = far_targets(core, topo)
+    if tg:
+        g.remote_dma_fused(
+            [RemoteDMATransfer(dst_ids=ids(tg), dma_engine_mask=0x00FF, remote_sem=S.far,
+                               srcs=[block], dsts=[block] * len(tg), alu_op=0)],
+            local_sem=S.sent)
+        sent += 8
+    g.wait_ge(S.far, 2 * 8)
+    g.wait_ge(S.sent, sent)
+
+    g.dma_start(T.y[:], T.land[:]).then_inc(S.stored, 16)
+    g.wait_ge(S.stored, 16)

@@ -2,24 +2,13 @@ from concourse.bass import RemoteDMATransfer, DstId
 
 SCRATCH = {
     "land": ("sbuf", [128, 192], "bfloat16"),
+    "xs": ("sbuf", [128, 8], "bfloat16"),
 }
 SEMAPHORES = ["loaded", "near", "far", "sent", "stored"]
 
 CHIPS = (0, 3, 5)
 SERVES = {2: (0, 1), 3: (2, 3), 6: (4, 5), 7: (6, 7)}
-
-
-def far_targets(core, topo):
-    ch, k = topo.chip(core), core % 8
-    out = []
-    for other in CHIPS:
-        if other == ch:
-            continue
-        if topo.same_plane(ch, other):
-            out.append(other * 8 + k)
-        elif k in SERVES:
-            out.extend(other * 8 + d for d in SERVES[k])
-    return out
+HANDS = {2: 0, 3: 1, 6: 4, 7: 5}
 
 
 def rank_program(g, core, T, topo):
@@ -27,32 +16,30 @@ def rank_program(g, core, T, topo):
     if rank is None:
         return
     S = T.sem
-    ch = topo.chip(core)
-    own = T.land[:, 8 * rank:8 * rank + 8]
+    ch, k = topo.chip(core), core % 8
+    carrier = k in SERVES
+    cols = T.land[:, 8 * rank:8 * rank + 8]
     b = rank // 8
     block = T.land[:, 64 * b:64 * b + 64]
 
-    def ids(cores):
-        return [DstId(rid=topo.addr(c)[0], pnc=topo.addr(c)[1]) for c in cores]
+    def tr(src, dst, cores, mask, sem):
+        return RemoteDMATransfer(dst_ids=[DstId(rid=topo.addr(c)[0], pnc=topo.addr(c)[1]) for c in cores],
+                                 dma_engine_mask=mask, remote_sem=sem,
+                                 srcs=[src], dsts=[dst] * len(cores), alu_op=0)
 
-    g.dma_start(own, T.x[:]).then_inc(S.loaded, 16)
+    mine = cols if carrier else T.xs[:]
+    g.dma_start(mine, T.x[:]).then_inc(S.loaded, 16)
     g.wait_ge(S.loaded, 16)
-    peers = [c for c in range(ch * 8, ch * 8 + 8) if c != core]
-    g.remote_dma_fused(
-        [RemoteDMATransfer(dst_ids=ids(peers), dma_engine_mask=0xFFFF, remote_sem=S.near,
-                           srcs=[own], dsts=[own] * len(peers), alu_op=0)],
-        local_sem=S.sent)
+    g.remote_dma_fused([tr(mine, cols, [ch * 8 + c for c in SERVES if c != k], 0xFFFF, S.near)], local_sem=S.sent)
     sent = 16
-    g.wait_ge(S.near, 7 * 16)
 
-    tg = far_targets(core, topo)
-    if tg:
-        g.remote_dma_fused(
-            [RemoteDMATransfer(dst_ids=ids(tg), dma_engine_mask=0x00FF, remote_sem=S.far,
-                               srcs=[block], dsts=[block] * len(tg), alu_op=0)],
-            local_sem=S.sent)
-        sent += 8
-    g.wait_ge(S.far, 2 * 8)
+    if carrier:
+        g.wait_ge(S.near, 7 * 16)
+        far = [o * 8 + d for o in CHIPS if o != ch for d in SERVES[k]]
+        g.remote_dma_fused([tr(block, block, far, 0x00FF, S.far),
+                            tr(block, block, [ch * 8 + HANDS[k]], 0xFF00, S.far)], local_sem=S.sent)
+        sent += 16
+    g.wait_ge(S.far, (2 if carrier else 3) * 8)
     g.wait_ge(S.sent, sent)
 
     g.dma_start(T.y[:], T.land[:]).then_inc(S.stored, 16)

@@ -9,35 +9,66 @@ SEMAPHORES = ["loaded", "near", "far", "sent", "stored"]
 CHIPS = (0, 3, 5)
 SERVES = {2: (0, 1), 3: (2, 3), 6: (4, 5), 7: (6, 7)}
 HANDS = {2: 0, 3: 1, 6: 4, 7: 5}
+HELPS = {
+    2 * 8 + 2: (0, [24 + d for d in (0, 1, 4, 5)]),
+    4 * 8 + 6: (0, [40 + d for d in (0, 1, 4, 5)]),
+    1 * 8 + 2: (5, [0, 1, 2, 3]),
+    1 * 8 + 6: (5, [4, 5, 6, 7]),
+}
+LO, HI, ALL = 0x00FF, 0xFF00, 0xFFFF
+
+
+def carrier_targets(ch, k):
+    if ch == 0:
+        return [24 + k, 40 + k]
+    if ch == 3:
+        return [d for d in SERVES[k]] + [40 + d for d in SERVES[k]]
+    return [24 + d for d in SERVES[k]]
 
 
 def rank_program(g, core, T, topo):
-    rank = T.rank_of(core)
-    if rank is None:
-        return
     S = T.sem
     ch, k = topo.chip(core), core % 8
-    carrier = k in SERVES
-    cols = T.land[:, 8 * rank:8 * rank + 8]
-    b = rank // 8
-    block = T.land[:, 64 * b:64 * b + 64]
+
+    def block(chip):
+        i = CHIPS.index(chip)
+        return T.land[:, 64 * i:64 * i + 64]
 
     def tr(src, dst, cores, mask, sem):
         return RemoteDMATransfer(dst_ids=[DstId(rid=topo.addr(c)[0], pnc=topo.addr(c)[1]) for c in cores],
                                  dma_engine_mask=mask, remote_sem=sem,
                                  srcs=[src], dsts=[dst] * len(cores), alu_op=0)
 
+    rank = T.rank_of(core)
+    if rank is None:
+        if core in HELPS:
+            frm, to = HELPS[core]
+            g.wait_ge(S.near, 8 * 8)
+            g.remote_dma_fused([tr(block(frm), block(frm), to, LO, S.far)], local_sem=S.sent)
+            g.wait_ge(S.sent, 8)
+        return
+
+    cols = T.land[:, 8 * rank:8 * rank + 8]
+    carrier = k in SERVES
+    helpers = [h for h in HELPS if HELPS[h][0] == ch]
+
     mine = cols if carrier else T.xs[:]
     g.dma_start(mine, T.x[:]).then_inc(S.loaded, 16)
     g.wait_ge(S.loaded, 16)
-    g.remote_dma_fused([tr(mine, cols, [ch * 8 + c for c in SERVES if c != k], 0xFFFF, S.near)], local_sem=S.sent)
+    inside = [ch * 8 + c for c in SERVES if c != k]
+    if helpers:
+        g.remote_dma_fused([tr(mine, cols, inside, HI, S.near), tr(mine, cols, helpers, LO, S.near)],
+                           local_sem=S.sent)
+        unit = 8
+    else:
+        g.remote_dma_fused([tr(mine, cols, inside, ALL, S.near)], local_sem=S.sent)
+        unit = 16
     sent = 16
 
     if carrier:
-        g.wait_ge(S.near, 7 * 16)
-        far = [o * 8 + d for o in CHIPS if o != ch for d in SERVES[k]]
-        g.remote_dma_fused([tr(block, block, far, 0x00FF, S.far),
-                            tr(block, block, [ch * 8 + HANDS[k]], 0xFF00, S.far)], local_sem=S.sent)
+        g.wait_ge(S.near, 7 * unit)
+        g.remote_dma_fused([tr(block(ch), block(ch), carrier_targets(ch, k), LO, S.far),
+                            tr(block(ch), block(ch), [ch * 8 + HANDS[k]], HI, S.far)], local_sem=S.sent)
         sent += 16
     g.wait_ge(S.far, (2 if carrier else 3) * 8)
     g.wait_ge(S.sent, sent)

@@ -10,8 +10,10 @@ CHIPS = (0, 3, 5)
 SERVES = {2: (0, 1), 3: (2, 3), 6: (4, 5), 7: (6, 7)}
 HANDS = {2: 0, 3: 1, 6: 4, 7: 5}
 HELPS = {
-    2 * 8 + 2: (0, [24 + d for d in (0, 1, 4, 5)]),
-    4 * 8 + 6: (0, [40 + d for d in (0, 1, 4, 5)]),
+    2 * 8 + 2: (0, [24 + d for d in (0, 1, 2)]),
+    2 * 8 + 6: (0, [24 + d for d in (4, 5, 6)]),
+    4 * 8 + 2: (0, [40 + d for d in (0, 1, 2)]),
+    4 * 8 + 6: (0, [40 + d for d in (4, 5, 6)]),
     1 * 8 + 2: (5, [0, 1, 2, 3]),
     1 * 8 + 6: (5, [4, 5, 6, 7]),
 }
@@ -20,7 +22,7 @@ LO, HI, ALL = 0x00FF, 0xFF00, 0xFFFF
 
 def carrier_targets(ch, k):
     if ch == 0:
-        return [24 + k, 40 + k]
+        return [{2: 27, 3: 43, 6: 31, 7: 47}[k]]
     if ch == 3:
         return [d for d in SERVES[k]] + [40 + d for d in SERVES[k]]
     return [24 + d for d in SERVES[k]]

from concourse.bass import RemoteDMATransfer, DstId

SCRATCH = {
    "land": ("sbuf", [128, 192], "bfloat16"),
    "xs": ("sbuf", [128, 8], "bfloat16"),
}
SEMAPHORES = ["loaded", "near", "far", "sent", "stored"]

CHIPS = (0, 3, 5)
SERVES = {2: (0, 1), 3: (2, 3), 6: (4, 5), 7: (6, 7)}
HANDS = {2: 0, 3: 1, 6: 4, 7: 5}
HELPS = {
    2 * 8 + 2: (0, [24 + d for d in (0, 1, 2)]),
    2 * 8 + 6: (0, [24 + d for d in (4, 5, 6)]),
    4 * 8 + 2: (0, [40 + d for d in (0, 1, 2)]),
    4 * 8 + 6: (0, [40 + d for d in (4, 5, 6)]),
    1 * 8 + 2: (5, [0, 1, 2, 3]),
    1 * 8 + 6: (5, [4, 5, 6, 7]),
}
LO, HI, ALL = 0x00FF, 0xFF00, 0xFFFF


def carrier_targets(ch, k):
    if ch == 0:
        return [{2: 27, 3: 43, 6: 31, 7: 47}[k]]
    if ch == 3:
        return [d for d in SERVES[k]] + [40 + d for d in SERVES[k]]
    return [24 + d for d in SERVES[k]]


def rank_program(g, core, T, topo):
    S = T.sem
    ch, k = topo.chip(core), core % 8

    def block(chip):
        i = CHIPS.index(chip)
        return T.land[:, 64 * i:64 * i + 64]

    def tr(src, dst, cores, mask, sem):
        return RemoteDMATransfer(dst_ids=[DstId(rid=topo.addr(c)[0], pnc=topo.addr(c)[1]) for c in cores],
                                 dma_engine_mask=mask, remote_sem=sem,
                                 srcs=[src], dsts=[dst] * len(cores), alu_op=0)

    rank = T.rank_of(core)
    if rank is None:
        if core in HELPS:
            frm, to = HELPS[core]
            g.wait_ge(S.near, 8 * 8)
            g.remote_dma_fused([tr(block(frm), block(frm), to, LO, S.far)], local_sem=S.sent)
            g.wait_ge(S.sent, 8)
        return

    cols = T.land[:, 8 * rank:8 * rank + 8]
    carrier = k in SERVES
    helpers = [h for h in HELPS if HELPS[h][0] == ch]

    mine = cols if carrier else T.xs[:]
    g.dma_start(mine, T.x[:]).then_inc(S.loaded, 16)
    g.wait_ge(S.loaded, 16)
    inside = [ch * 8 + c for c in SERVES if c != k]
    if helpers:
        g.remote_dma_fused([tr(mine, cols, inside, HI, S.near), tr(mine, cols, helpers, LO, S.near)],
                           local_sem=S.sent)
        unit = 8
    else:
        g.remote_dma_fused([tr(mine, cols, inside, ALL, S.near)], local_sem=S.sent)
        unit = 16
    sent = 16

    if carrier:
        g.wait_ge(S.near, 7 * unit)
        g.remote_dma_fused([tr(block(ch), block(ch), carrier_targets(ch, k), LO, S.far),
                            tr(block(ch), block(ch), [ch * 8 + HANDS[k]], HI, S.far)], local_sem=S.sent)
        sent += 16
    g.wait_ge(S.far, (2 if carrier else 3) * 8)
    g.wait_ge(S.sent, sent)

    g.dma_start(T.y[:], T.land[:]).then_inc(S.stored, 16)
    g.wait_ge(S.stored, 16)
